import numpy as np
import ml_dtypes


def mxq(x, axis, fmt="e4m3"):
    dtype, down = {"e4m3": (ml_dtypes.float8_e4m3fn, 7), "e5m2": (ml_dtypes.float8_e5m2, 14)}[fmt]
    v = np.moveaxis(np.asarray(x, np.float32).astype(ml_dtypes.bfloat16).astype(np.float64), axis, -1)
    blocks = v.reshape(v.shape[:-1] + (-1, 32))
    amax = np.abs(blocks).max(-1, keepdims=True)
    byte = np.maximum(np.where(amax > 0, np.frexp(amax)[1] - 1 + 127, 0) - down, 1)
    scale = np.exp2(byte - 127.0)
    codes = (blocks / scale).astype(np.float32).astype(dtype).astype(np.float64)
    return np.moveaxis((codes * scale).reshape(v.shape), -1, axis)


WIDE = False


def mx_kscale(k):
    if not WIDE:
        return np.ones(k)
    levels = np.array([10, -10, 5, -5, 0])
    if k % 512:
        return np.exp2(np.random.permutation(np.resize(levels, k // 32))).repeat(32)
    a = np.empty((k // 512, 16))
    for p in range(k // 512):
        a[p, :8] = np.random.permutation(np.resize(levels, 8))
        for g in range(8):
            far = levels[np.abs(levels - a[p, g]) >= 10]
            a[p, g + 8] = far[np.random.randint(len(far))]
    return np.exp2(a.ravel()).repeat(32)


def f64(x):
    return np.asarray(x).astype(np.float64)


def split(x):
    m, e = np.frexp(f64(x))
    hi = np.ldexp(np.trunc(16.0 * m) / 16.0, e)
    return hi, f64(x) - hi


K, M, T = 2048, 512, 1024


def setup_inputs():
    n = np.random.standard_normal
    s = mx_kscale(K)[:, None]
    return {
        "w": (n((K, M)) / np.sqrt(K) / s).astype(np.float32),
        "x": (n((K, T)) * s).astype(np.float32),
        "b": (0.3 * n(512)).astype(np.float32),
    }


def reference(w, x, b):
    w_hi, w_lo = split(w)
    w_hi_, w_lo_ = mxq(w_hi, 0, "e4m3"), mxq(w_lo, 0, "e4m3")
    x_hi, x_lo = split(x)
    x_hi_, x_lo_ = mxq(x_hi, 0, "e4m3"), mxq(x_lo, 0, "e4m3")
    y = w_hi_.T @ x_hi_ + w_hi_.T @ x_lo_ + w_lo_.T @ x_hi_
    return y + f64(b)[:, None]

@@ -1,0 +1,175 @@
+from contextlib import ExitStack
+
+import concourse.mybir as mybir
+
+K, M, T = 2048, 512, 1024
+FLOPS = 3 * 2 * K * M * T
+
+F32 = mybir.dt.float32
+BF16 = mybir.dt.bfloat16
+I32 = mybir.dt.int32
+U32 = mybir.dt.uint32
+U8 = mybir.dt.uint8
+FP8X4 = mybir.dt.float8_e4m3fn_x4
+ALU = mybir.AluOpType
+ACT = mybir.ActivationFunctionType
+
+P = 128
+PACK = 4
+K_PASS = P * PACK
+PASSES = K // K_PASS
+M_TILES = M // P
+HALF = 512
+QUARTER = 256
+HI_MASK = 0xFFF0FFF0 - 2**32
+
+
+def tile_mix_split3_fm_bias_kernel(tc, w, x, b, out):
+    nc = tc.nc
+    with ExitStack() as ctx:
+        ctx.enter_context(tc.manual_schedule())
+        keep = ctx.enter_context(tc.tile_pool(name="keep", bufs=1))
+        group = ctx.enter_context(tc.tile_pool(name="group", bufs=4))
+        outs = ctx.enter_context(tc.tile_pool(name="outs", bufs=1))
+        psum = ctx.enter_context(tc.psum_pool(name="psum", bufs=1))
+
+        warm_in = keep.tile([P, 8], F32, name="warm_in")
+        warm_out = keep.tile([P, 8], F32, name="warm_out")
+        nc.vector.memset(warm_in[:], 0.0)
+        nc.scalar.activation(warm_out[:], warm_in[:], ACT.Identity)
+
+        units = [("w", 0, 0, 128), ("w", 0, 128, 128), ("w", 0, 256, 256), ("x", 0, 0, HALF)]
+        for c in range(1, PASSES):
+            units.append(("w", c, 0, HALF))
+            units.append(("x", c, 0, HALF))
+        for c in range(PASSES - 1):
+            units.append(("x", c, HALF, HALF))
+        units.append(("x", PASSES - 1, HALF, QUARTER))
+        units.append(("x", PASSES - 1, HALF + QUARTER, QUARTER))
+
+        dram = {"w": w, "x": x}
+        bias = keep.tile([P, M_TILES], F32, name="bias")
+        raws = []
+        for n, (src, c, c0, width) in enumerate(units):
+            raw = keep.tile([P, PACK, width], F32, name="raw_%d" % n)
+            rows = dram[src][c * K_PASS : (c + 1) * K_PASS, c0 : c0 + width]
+            nc.sync.dma_start(out=raw[:], in_=rows.rearrange("(p j) w -> p j w", j=PACK))
+            raws.append(raw)
+            if n == 7:
+                with nc.allow_non_contiguous_dma(reason="bias onto partitions"):
+                    nc.sync.dma_start(out=bias[:], in_=b.rearrange("(m p) -> p m", p=P))
+
+        codes = {}
+        scales = {}
+        for src, cols in (("w", M), ("x", T)):
+            for part in ("hi", "lo"):
+                for c in range(PASSES):
+                    codes[src, part, c] = keep.tile([P, cols], U32, name="codes_%s_%s_%d" % (src, part, c), align_bytes=64)
+                    scales[src, part, c] = keep.tile([P, cols], U8, name="scales_%s_%s_%d" % (src, part, c), align_bytes=64)
+
+        his = {}
+        los = {}
+
+        def by_column(ap):
+            return ap.rearrange("p (c i t) -> p c t i", t=PACK, i=4)
+
+        def upper_halves(u):
+            width = units[u][3]
+            hi = group.tile([P, HALF * PACK], BF16, name="hi", align_bytes=64)
+            his[u] = hi
+            words = raws[u][:].rearrange("p t w -> p (t w)").bitcast(BF16)
+            src = words.rearrange("p (t c i e) -> p c t i e", t=PACK, i=4, e=2)[:, :, :, :, 1]
+            nc.scalar.copy(out=by_column(hi[:, : width * PACK]), in_=src)
+
+        def mask(u):
+            bits = his[u][:, : units[u][3] * PACK].bitcast(I32)
+            nc.vector.tensor_scalar(out=bits, in0=bits, scalar1=HI_MASK, scalar2=None, op0=ALU.bitwise_and)
+
+        def low(u, parts):
+            width = units[u][3]
+            lo = group.tile([P, HALF * PACK], BF16, name="lo", align_bytes=64)
+            los[u] = lo
+            step = width // parts
+            for s in range(0, width, step):
+                cols = slice(s * PACK, (s + step) * PACK)
+                nc.vector.tensor_tensor(
+                    out=by_column(lo[:, cols]),
+                    in0=raws[u][:, :, s : s + step].rearrange("p t (c i) -> p c t i", i=4),
+                    in1=by_column(his[u][:, cols]),
+                    op=ALU.subtract,
+                )
+
+        def quantize(u, part, parts):
+            src, c, c0, width = units[u]
+            tile = (his if part == "hi" else los)[u]
+            step = width // parts
+            for s in range(0, width, step):
+                dst = slice(c0 + s, c0 + s + step)
+                nc.vector.quantize_mx(
+                    out=codes[src, part, c][:, dst].bitcast(FP8X4),
+                    scales=scales[src, part, c][:, dst],
+                    in_=tile[:, s * PACK : (s + step) * PACK],
+                )
+
+        banks = {}
+
+        def open_banks(c0, width, tag):
+            for m in range(M_TILES):
+                banks[c0, m] = psum.tile([P, width], F32, name="bank_%s%d" % (tag, m))
+
+        def multiply(u, pairs, first, last):
+            src, c, c0, width = units[u]
+            if src == "w":
+                return
+            n = HALF if c0 == 0 else QUARTER
+            for n0 in range(c0, c0 + width, n):
+                for m in range(M_TILES):
+                    for i, (wp, xp) in enumerate(pairs):
+                        nc.tensor.matmul_mx(
+                            out=banks[n0, m][:],
+                            lhsT=codes["w", wp, c][:, m * P : (m + 1) * P].bitcast(FP8X4),
+                            lhsT_scale=scales["w", wp, c][:, m * P : (m + 1) * P],
+                            rhs=codes["x", xp, c][:, n0 : n0 + n].bitcast(FP8X4),
+                            rhs_scale=scales["x", xp, c][:, n0 : n0 + n],
+                            start=(first and c == 0 and i == 0),
+                            stop=(last and c == PASSES - 1 and i == len(pairs) - 1),
+                        )
+
+        def drain(c0, width, vector_tiles):
+            for m in range(M_TILES):
+                res = outs.tile([P, width], F32, name="res_%d_%d" % (c0, m))
+                if m in vector_tiles:
+                    nc.vector.tensor_scalar(out=res[:], in0=banks[c0, m][:], scalar1=bias[:, m : m + 1], scalar2=None, op0=ALU.add)
+                else:
+                    nc.scalar.activation(res[:], banks[c0, m][:], ACT.Identity, bias=bias[:, m : m + 1])
+                nc.sync.dma_start(out=out[m * P : (m + 1) * P, c0 : c0 + width], in_=res[:])
+
+        def after_low(u):
+            multiply(u, [("hi", "lo")], False, True)
+            src, c, c0, width = units[u]
+            if src == "x" and c == PASSES - 1:
+                if c0 == 0:
+                    drain(0, HALF, ())
+                    open_banks(HALF + QUARTER, QUARTER, "a")
+                elif c0 == HALF:
+                    drain(HALF, QUARTER, ())
+                else:
+                    drain(HALF + QUARTER, QUARTER, (1, 3))
+
+        open_banks(0, HALF, "a")
+        open_banks(HALF, QUARTER, "b")
+        n_units = len(units)
+        upper_halves(0)
+        upper_halves(1)
+        for u in range(n_units):
+            if u + 2 < n_units:
+                upper_halves(u + 2)
+            mask(u)
+            if u > 0:
+                quantize(u - 1, "lo", 1)
+                after_low(u - 1)
+            quantize(u, "hi", 1)
+            multiply(u, [("hi", "hi"), ("lo", "hi")], True, False)
+            low(u, 2 if u == n_units - 1 else 1)
+        quantize(n_units - 1, "lo", 2)
+        after_low(n_units - 1)

@@ -1,6 +1,7 @@
 from contextlib import ExitStack
 
 import concourse.mybir as mybir
+from concourse.masks import make_identity
 
 K, M, T = 2048, 512, 1024
 FLOPS = 3 * 2 * K * M * T
@@ -21,7 +22,28 @@ PASSES = K // K_PASS
 M_TILES = M // P
 HALF = 512
 QUARTER = 256
-HI_MASK = 0xFFF0FFF0 - 2**32
+MASK_PAIR = 0xFFF0FFF0 - 2**32
+MASK_F32 = 0xFFF00000 - 2**32
+SIGN = -(2**31)
+ROUTED = {7: 256, 8: 384}
+AHEAD = {7: 2, 8: 2}
+
+GROUPS = (
+    (("w", 0, 0, 128),),
+    (("w", 0, 128, 128),),
+    (("w", 0, 256, 256),),
+    (("x", 0, 0, 256),),
+    (("x", 0, 256, 256),),
+    (("w", 1, 0, 512),),
+    (("x", 1, 0, 512),),
+    (("w", 2, 0, 512), ("x", 2, 0, 512)),
+    (("w", 3, 0, 512), ("x", 3, 0, 512)),
+    (("x", 0, 512, 512),),
+    (("x", 1, 512, 512),),
+    (("x", 2, 512, 512),),
+    (("x", 3, 512, 256),),
+    (("x", 3, 768, 256),),
+)
 
 
 def tile_mix_split3_fm_bias_kernel(tc, w, x, b, out):
@@ -29,8 +51,8 @@ def tile_mix_split3_fm_bias_kernel(tc, w, x, b, out):
     with ExitStack() as ctx:
         ctx.enter_context(tc.manual_schedule())
         keep = ctx.enter_context(tc.tile_pool(name="keep", bufs=1))
-        group = ctx.enter_context(tc.tile_pool(name="group", bufs=4))
-        outs = ctx.enter_context(tc.tile_pool(name="outs", bufs=1))
+        his = ctx.enter_context(tc.tile_pool(name="his", bufs=3))
+        los = ctx.enter_context(tc.tile_pool(name="los", bufs=2))
         psum = ctx.enter_context(tc.psum_pool(name="psum", bufs=1))
 
         warm_in = keep.tile([P, 8], F32, name="warm_in")
@@ -38,77 +60,140 @@ def tile_mix_split3_fm_bias_kernel(tc, w, x, b, out):
         nc.vector.memset(warm_in[:], 0.0)
         nc.scalar.activation(warm_out[:], warm_in[:], ACT.Identity)
 
-        units = [("w", 0, 0, 128), ("w", 0, 128, 128), ("w", 0, 256, 256), ("x", 0, 0, HALF)]
-        for c in range(1, PASSES):
-            units.append(("w", c, 0, HALF))
-            units.append(("x", c, 0, HALF))
-        for c in range(PASSES - 1):
-            units.append(("x", c, HALF, HALF))
-        units.append(("x", PASSES - 1, HALF, QUARTER))
-        units.append(("x", PASSES - 1, HALF + QUARTER, QUARTER))
+        eye_f32 = keep.tile([P, P], F32, name="eye_f32")
+        eye_bf16 = keep.tile([P, P], BF16, name="eye_bf16")
+        make_identity(nc, eye_f32[:])
+        make_identity(nc, eye_bf16[:])
 
-        dram = {"w": w, "x": x}
         bias = keep.tile([P, M_TILES], F32, name="bias")
-        raws = []
-        for n, (src, c, c0, width) in enumerate(units):
-            raw = keep.tile([P, PACK, width], F32, name="raw_%d" % n)
-            rows = dram[src][c * K_PASS : (c + 1) * K_PASS, c0 : c0 + width]
-            nc.sync.dma_start(out=raw[:], in_=rows.rearrange("(p j) w -> p j w", j=PACK))
-            raws.append(raw)
-            if n == 7:
+        raw = {}
+        for block in [block for group in GROUPS for block in group]:
+            src, c, c0, width = block
+            if block == ("x", 2, HALF, HALF):
                 with nc.allow_non_contiguous_dma(reason="bias onto partitions"):
                     nc.sync.dma_start(out=bias[:], in_=b.rearrange("(m p) -> p m", p=P))
+            raw[block] = keep.tile([P, PACK, width], F32, name="raw_%s_%d_%d" % (src, c, c0))
+            rows = (w if src == "w" else x)[c * K_PASS : (c + 1) * K_PASS, c0 : c0 + width]
+            nc.sync.dma_start(out=raw[block][:], in_=rows.rearrange("(p j) w -> p j w", j=PACK))
 
-        codes = {}
-        scales = {}
-        for src, cols in (("w", M), ("x", T)):
-            for part in ("hi", "lo"):
-                for c in range(PASSES):
-                    codes[src, part, c] = keep.tile([P, cols], U32, name="codes_%s_%s_%d" % (src, part, c), align_bytes=64)
-                    scales[src, part, c] = keep.tile([P, cols], U8, name="scales_%s_%s_%d" % (src, part, c), align_bytes=64)
+        codes, scales = {}, {}
+        for c in range(PASSES):
+            for side, cols in (("left", M + HALF), ("right", HALF)):
+                for part in ("hi", "lo"):
+                    tag = "%s_%s_%d" % (side, part, c)
+                    codes[side, part, c] = keep.tile([P, cols], U32, name="codes_" + tag, align_bytes=64)
+                    scales[side, part, c] = keep.tile([P, cols], U8, name="scales_" + tag, align_bytes=64)
 
-        his = {}
-        los = {}
+        def home(block):
+            src, c, c0, width = block
+            if src == "w":
+                return "left", c0
+            return ("left", M + c0) if c0 < HALF else ("right", c0 - HALF)
 
-        def by_column(ap):
-            return ap.rearrange("p (c i t) -> p c t i", t=PACK, i=4)
+        full_hi = keep.tile([P, PACK, GROUPS[0][0][3]], F32, name="full_hi")
+        hi, lo = {}, {}
 
-        def upper_halves(u):
-            width = units[u][3]
-            hi = group.tile([P, HALF * PACK], BF16, name="hi", align_bytes=64)
-            his[u] = hi
-            words = raws[u][:].rearrange("p t w -> p (t w)").bitcast(BF16)
-            src = words.rearrange("p (t c i e) -> p c t i e", t=PACK, i=4, e=2)[:, :, :, :, 1]
-            nc.scalar.copy(out=by_column(hi[:, : width * PACK]), in_=src)
+        def runs(ap, run):
+            return ap.rearrange("p t (c i) -> p c t i", i=run)
 
-        def mask(u):
-            bits = his[u][:, : units[u][3] * PACK].bitcast(I32)
-            nc.vector.tensor_scalar(out=bits, in0=bits, scalar1=HI_MASK, scalar2=None, op0=ALU.bitwise_and)
+        def packed(tile, start, width, run):
+            return tile[:, start * PACK : (start + width) * PACK].rearrange("p (c i t) -> p c t i", t=PACK, i=run)
 
-        def low(u, parts):
-            width = units[u][3]
-            lo = group.tile([P, HALF * PACK], BF16, name="lo", align_bytes=64)
-            los[u] = lo
-            step = width // parts
-            for s in range(0, width, step):
-                cols = slice(s * PACK, (s + step) * PACK)
-                nc.vector.tensor_tensor(
-                    out=by_column(lo[:, cols]),
-                    in0=raws[u][:, :, s : s + step].rearrange("p t (c i) -> p c t i", i=4),
-                    in1=by_column(his[u][:, cols]),
-                    op=ALU.subtract,
+        def routed(g):
+            return ROUTED.get(g, 0)
+
+        def halves_of(full):
+            halves = full[:].rearrange("p t w -> p (t w)").bitcast(BF16)
+            return halves.rearrange("p (t w e) -> p t w e", t=PACK, e=2)[:, :, :, 1]
+
+        def copies(g):
+            todo = []
+            hi[g] = his.tile([P, 2 * HALF * PACK], BF16, name="hi", align_bytes=64)
+            start = 0
+            for block in GROUPS[g]:
+                width = block[3]
+                full = full_hi if g == 0 else raw[block]
+                skip = routed(g) if start == 0 else 0
+                step = min(QUARTER, width - skip) if skip or g == 9 else width
+                for s in range(skip, width, step):
+                    todo.append((packed(hi[g], start + s, step, 4), runs(halves_of(full)[:, :, s : s + step], 4)))
+                start += width
+            return todo
+
+        def copy_upper_halves(g):
+            for dst, src in copies(g):
+                nc.scalar.copy(out=dst, in_=src)
+
+        negative, flipped, low_t, low_p = {}, {}, {}, {}
+
+        def negate_routed(g):
+            negative[g] = keep.tile([P, PACK, routed(g)], F32, name="negative_%d" % (g % 2))
+            nc.vector.tensor_scalar(
+                out=negative[g][:].bitcast(I32), in0=raw[GROUPS[g][0]][:, :, : routed(g)].bitcast(I32),
+                scalar1=MASK_F32, scalar2=SIGN, op0=ALU.bitwise_and, op1=ALU.bitwise_xor,
+            )
+
+        def route_there(g):
+            for s in range(0, routed(g), P):
+                flipped[g, s] = psum.tile([P, PACK * P], F32, name="bank_b%d" % (s // P))
+                for t in range(PACK):
+                    for source, first in ((raw[GROUPS[g][0]], True), (negative[g], False)):
+                        nc.tensor.matmul(
+                            flipped[g, s][:, t * P : (t + 1) * P], lhsT=source[:, t, s : s + P], rhs=eye_f32[:],
+                            start=first, stop=not first, is_transpose=True,
+                        )
+            nc.scalar.activation(packed(hi[g], 0, routed(g), 4), runs(halves_of(negative[g]), 4), ACT.Copy, scale=-1.0)
+
+        def route_back(g):
+            for s in range(0, routed(g), P):
+                low_t[g, s] = keep.tile([P, PACK * P], BF16, name="low_t_%d" % s)
+                nc.scalar.copy(out=low_t[g, s][:], in_=flipped[g, s][:])
+            for s in range(0, routed(g), P):
+                low_p[g, s] = psum.tile([P, PACK, P], BF16, name="bank_b%d" % ((s // P + max(2, routed(g) // P)) % 4))
+                for t in range(PACK):
+                    nc.tensor.transpose(low_p[g, s][:, t, :], low_t[g, s][:, t * P : (t + 1) * P], eye_bf16[:])
+
+        def route_end(g):
+            for s in range(0, routed(g), P):
+                nc.scalar.copy(
+                    out=lo[g][:, s * PACK : (s + P) * PACK].rearrange("p (c t) -> p c t", t=PACK),
+                    in_=low_p[g, s][:].rearrange("p t c -> p c t"),
                 )
 
-        def quantize(u, part, parts):
-            src, c, c0, width = units[u]
-            tile = (his if part == "hi" else los)[u]
+        def mask_first():
+            nc.vector.tensor_scalar(
+                out=full_hi[:].bitcast(I32), in0=raw[GROUPS[0][0]][:].bitcast(I32), scalar1=MASK_F32, scalar2=None, op0=ALU.bitwise_and
+            )
+
+        def mask(g):
+            width = sum(block[3] for block in GROUPS[g])
+            bits = hi[g][:, routed(g) * PACK : width * PACK].bitcast(I32)
+            nc.vector.tensor_scalar(out=bits, in0=bits, scalar1=MASK_PAIR, scalar2=None, op0=ALU.bitwise_and)
+
+        def subtract(g, i, parts):
+            if i == 0:
+                lo[g] = los.tile([P, 2 * HALF * PACK], BF16, name="lo", align_bytes=64)
+            block = GROUPS[g][i]
+            begin = sum(other[3] for other in GROUPS[g][:i])
+            skip = routed(g) if i == 0 else 0
+            step = (block[3] - skip) // parts
+            for s in range(skip, block[3], step):
+                minus = runs(full_hi[:], 2) if g == 0 else packed(hi[g], begin + s, step, 2)
+                nc.vector.tensor_tensor(
+                    out=packed(lo[g], begin + s, step, 2), in0=runs(raw[block][:, :, s : s + step], 2), in1=minus, op=ALU.subtract
+                )
+
+        def quantize(tile, part, blocks, start, parts=1):
+            side, col = home(blocks[0])
+            c = blocks[0][1]
+            width = sum(block[3] for block in blocks)
             step = width // parts
             for s in range(0, width, step):
-                dst = slice(c0 + s, c0 + s + step)
+                dst = slice(col + s, col + s + step)
                 nc.vector.quantize_mx(
-                    out=codes[src, part, c][:, dst].bitcast(FP8X4),
-                    scales=scales[src, part, c][:, dst],
-                    in_=tile[:, s * PACK : (s + step) * PACK],
+                    out=codes[side, part, c][:, dst].bitcast(FP8X4),
+                    scales=scales[side, part, c][:, dst],
+                    in_=tile[:, (start + s) * PACK : (start + s + step) * PACK],
                 )
 
         banks = {}
@@ -117,59 +202,98 @@ def tile_mix_split3_fm_bias_kernel(tc, w, x, b, out):
             for m in range(M_TILES):
                 banks[c0, m] = psum.tile([P, width], F32, name="bank_%s%d" % (tag, m))
 
-        def multiply(u, pairs, first, last):
-            src, c, c0, width = units[u]
-            if src == "w":
-                return
-            n = HALF if c0 == 0 else QUARTER
-            for n0 in range(c0, c0 + width, n):
+        def multiply(block, pairs):
+            src, c, c0, width = block
+            if c0 < HALF:
+                starts, n = [0] if c0 + width == HALF else [], HALF
+            else:
+                starts, n = range(c0, c0 + width, QUARTER), QUARTER
+            for n0 in starts:
+                side, col = home(("x", c, n0, n))
                 for m in range(M_TILES):
-                    for i, (wp, xp) in enumerate(pairs):
+                    w_cols = slice(m * P, (m + 1) * P)
+                    x_cols = slice(col, col + n)
+                    for w_part, x_part in pairs:
                         nc.tensor.matmul_mx(
                             out=banks[n0, m][:],
-                            lhsT=codes["w", wp, c][:, m * P : (m + 1) * P].bitcast(FP8X4),
-                            lhsT_scale=scales["w", wp, c][:, m * P : (m + 1) * P],
-                            rhs=codes["x", xp, c][:, n0 : n0 + n].bitcast(FP8X4),
-                            rhs_scale=scales["x", xp, c][:, n0 : n0 + n],
-                            start=(first and c == 0 and i == 0),
-                            stop=(last and c == PASSES - 1 and i == len(pairs) - 1),
+                            lhsT=codes["left", w_part, c][:, w_cols].bitcast(FP8X4),
+                            lhsT_scale=scales["left", w_part, c][:, w_cols],
+                            rhs=codes[side, x_part, c][:, x_cols].bitcast(FP8X4),
+                            rhs_scale=scales[side, x_part, c][:, x_cols],
+                            start=(c == 0 and (w_part, x_part) == ("hi", "hi")),
+                            stop=(c == PASSES - 1 and (w_part, x_part) == ("hi", "lo")),
                         )
 
         def drain(c0, width, vector_tiles):
             for m in range(M_TILES):
-                res = outs.tile([P, width], F32, name="res_%d_%d" % (c0, m))
+                res = keep.tile([P, width], F32, name="res_%d_%d" % (c0, m))
                 if m in vector_tiles:
                     nc.vector.tensor_scalar(out=res[:], in0=banks[c0, m][:], scalar1=bias[:, m : m + 1], scalar2=None, op0=ALU.add)
                 else:
                     nc.scalar.activation(res[:], banks[c0, m][:], ACT.Identity, bias=bias[:, m : m + 1])
                 nc.sync.dma_start(out=out[m * P : (m + 1) * P, c0 : c0 + width], in_=res[:])
 
-        def after_low(u):
-            multiply(u, [("hi", "lo")], False, True)
-            src, c, c0, width = units[u]
-            if src == "x" and c == PASSES - 1:
-                if c0 == 0:
-                    drain(0, HALF, ())
-                    open_banks(HALF + QUARTER, QUARTER, "a")
-                elif c0 == HALF:
-                    drain(HALF, QUARTER, ())
-                else:
-                    drain(HALF + QUARTER, QUARTER, (1, 3))
+        def finish_low(g, parts=1):
+            block = GROUPS[g][-1]
+            quantize(lo[g], "lo", [block], sum(other[3] for other in GROUPS[g][:-1]), parts)
+            if block[0] == "x":
+                multiply(block, [("hi", "lo")])
+                if block[1] == PASSES - 1:
+                    if block[2] == 0:
+                        drain(0, HALF, ())
+                        open_banks(HALF + QUARTER, QUARTER, "a")
+                        open_banks(HALF, QUARTER, "b")
+                    elif block[2] == HALF:
+                        drain(HALF, QUARTER, ())
+                    else:
+                        drain(HALF + QUARTER, QUARTER, (1, 3))
 
         open_banks(0, HALF, "a")
-        open_banks(HALF, QUARTER, "b")
-        n_units = len(units)
-        upper_halves(0)
-        upper_halves(1)
-        for u in range(n_units):
-            if u + 2 < n_units:
-                upper_halves(u + 2)
-            mask(u)
-            if u > 0:
-                quantize(u - 1, "lo", 1)
-                after_low(u - 1)
-            quantize(u, "hi", 1)
-            multiply(u, [("hi", "hi"), ("lo", "hi")], True, False)
-            low(u, 2 if u == n_units - 1 else 1)
-        quantize(n_units - 1, "lo", 2)
-        after_low(n_units - 1)
+        last = len(GROUPS) - 1
+        mask_first()
+        copy_upper_halves(0)
+        copy_upper_halves(1)
+        copy_upper_halves(2)
+        subtract(0, 0, 1)
+        quantize(hi[0], "hi", GROUPS[0], 0)
+        for g in range(1, last + 1):
+            pair = len(GROUPS[g]) == 2
+            block = GROUPS[g][-1]
+            ahead = []
+            if routed(g):
+                if g not in negative:
+                    negate_routed(g)
+                    route_there(g)
+                ahead = copies(max(hi) + 1) if max(hi) < g + 2 else []
+            elif g + 2 <= last and g != 9 and g + 2 not in hi and not (routed(g + 1) and g + 2 > 6):
+                if not (g == 5 and routed(7) and False):
+                    copy_upper_halves(g + 2)
+            elif g == 9:
+                copy_upper_halves(10)
+            mask(g)
+            finish_low(g - 1)
+            if g == 9:
+                copy_upper_halves(11)
+            if routed(g):
+                route_back(g)
+                for dst, src in ahead[: AHEAD[g]]:
+                    nc.scalar.copy(out=dst, in_=src)
+                subtract(g, 0, 1)
+                route_end(g)
+                for dst, src in ahead[AHEAD[g] :]:
+                    nc.scalar.copy(out=dst, in_=src)
+            if g < last and routed(g + 1):
+                negate_routed(g + 1)
+                route_there(g + 1)
+            quantize(hi[g], "hi", GROUPS[g], 0)
+            if block[0] == "x":
+                multiply(block, [("hi", "hi")] if pair else [("hi", "hi"), ("lo", "hi")])
+            if pair:
+                if not routed(g):
+                    subtract(g, 0, 1)
+                subtract(g, 1, 1)
+                quantize(lo[g], "lo", GROUPS[g][:1], 0)
+                multiply(block, [("lo", "hi")])
+            elif not routed(g):
+                subtract(g, 0, 2 if g == last else 1)
+        finish_low(last, 2)

@@ -20,15 +20,14 @@ PACK = 4
 K_PASS = P * PACK
 PASSES = K // K_PASS
 M_TILES = M // P
-HALF = 512
-QUARTER = 256
-MASK_PAIR = 0xFFF0FFF0 - 2**32
-MASK_F32 = 0xFFF00000 - 2**32
-SIGN = -(2**31)
-ROUTED = {7: 256, 8: 384}
-AHEAD = {7: 2, 8: 2}
+HALF = T // 2
+QUARTER = T // 4
 
-GROUPS = (
+MASK_F32 = 0xFFF00000 - 2**32
+MASK_BF16_PAIR = 0xFFF0FFF0 - 2**32
+SIGN_F32 = -(2**31)
+
+STEPS = (
     (("w", 0, 0, 128),),
     (("w", 0, 128, 128),),
     (("w", 0, 256, 256),),
@@ -44,6 +43,39 @@ GROUPS = (
     (("x", 3, 512, 256),),
     (("x", 3, 768, 256),),
 )
+LAST = len(STEPS) - 1
+DETOUR = 256
+BIAS_AHEAD_OF = ("x", 2, 512, 512)
+COPY_RUN = 4
+SUBTRACT_RUN = 2
+
+
+def takes_detour(step):
+    return step <= LAST and len(STEPS[step]) == 2
+
+
+def columns(blocks):
+    return sum(block[3] for block in blocks)
+
+
+def home(block):
+    operand, first = block[0], block[2]
+    if operand == "w":
+        return "left", first
+    return ("left", M + first) if first < HALF else ("right", first - HALF)
+
+
+def by_runs(rows, run):
+    return rows.rearrange("p t (c i) -> p c t i", i=run)
+
+
+def packed_by_runs(tile, start, width, run):
+    return tile[:, start * PACK : (start + width) * PACK].rearrange("p (c i t) -> p c t i", t=PACK, i=run)
+
+
+def upper_halves(full):
+    halves = full[:].rearrange("p t w -> p (t w)").bitcast(BF16)
+    return halves.rearrange("p (t w e) -> p t w e", t=PACK, e=2)[:, :, :, 1]
 
 
 def tile_mix_split3_fm_bias_kernel(tc, w, x, b, out):
@@ -55,10 +87,10 @@ def tile_mix_split3_fm_bias_kernel(tc, w, x, b, out):
         los = ctx.enter_context(tc.tile_pool(name="los", bufs=2))
         psum = ctx.enter_context(tc.psum_pool(name="psum", bufs=1))
 
-        warm_in = keep.tile([P, 8], F32, name="warm_in")
-        warm_out = keep.tile([P, 8], F32, name="warm_out")
-        nc.vector.memset(warm_in[:], 0.0)
-        nc.scalar.activation(warm_out[:], warm_in[:], ACT.Identity)
+        table_in = keep.tile([P, 8], F32, name="table_in")
+        table_out = keep.tile([P, 8], F32, name="table_out")
+        nc.vector.memset(table_in[:], 0.0)
+        nc.scalar.activation(table_out[:], table_in[:], ACT.Identity)
 
         eye_f32 = keep.tile([P, P], F32, name="eye_f32")
         eye_bf16 = keep.tile([P, P], BF16, name="eye_bf16")
@@ -67,233 +99,207 @@ def tile_mix_split3_fm_bias_kernel(tc, w, x, b, out):
 
         bias = keep.tile([P, M_TILES], F32, name="bias")
         raw = {}
-        for block in [block for group in GROUPS for block in group]:
-            src, c, c0, width = block
-            if block == ("x", 2, HALF, HALF):
-                with nc.allow_non_contiguous_dma(reason="bias onto partitions"):
+        for block in [block for blocks in STEPS for block in blocks]:
+            operand, c, first, width = block
+            if block == BIAS_AHEAD_OF:
+                with nc.allow_non_contiguous_dma(reason="one bias value to a partition"):
                     nc.sync.dma_start(out=bias[:], in_=b.rearrange("(m p) -> p m", p=P))
-            raw[block] = keep.tile([P, PACK, width], F32, name="raw_%s_%d_%d" % (src, c, c0))
-            rows = (w if src == "w" else x)[c * K_PASS : (c + 1) * K_PASS, c0 : c0 + width]
+            raw[block] = keep.tile([P, PACK, width], F32, name="raw_%s_%d_%d" % (operand, c, first))
+            rows = (w if operand == "w" else x)[c * K_PASS : (c + 1) * K_PASS, first : first + width]
             nc.sync.dma_start(out=raw[block][:], in_=rows.rearrange("(p j) w -> p j w", j=PACK))
 
         codes, scales = {}, {}
         for c in range(PASSES):
-            for side, cols in (("left", M + HALF), ("right", HALF)):
+            for side, width in (("left", M + HALF), ("right", HALF)):
                 for part in ("hi", "lo"):
                     tag = "%s_%s_%d" % (side, part, c)
-                    codes[side, part, c] = keep.tile([P, cols], U32, name="codes_" + tag, align_bytes=64)
-                    scales[side, part, c] = keep.tile([P, cols], U8, name="scales_" + tag, align_bytes=64)
+                    codes[side, part, c] = keep.tile([P, width], U32, name="codes_" + tag, align_bytes=64)
+                    scales[side, part, c] = keep.tile([P, width], U8, name="scales_" + tag, align_bytes=64)
 
-        def home(block):
-            src, c, c0, width = block
-            if src == "w":
-                return "left", c0
-            return ("left", M + c0) if c0 < HALF else ("right", c0 - HALF)
-
-        full_hi = keep.tile([P, PACK, GROUPS[0][0][3]], F32, name="full_hi")
         hi, lo = {}, {}
 
-        def runs(ap, run):
-            return ap.rearrange("p t (c i) -> p c t i", i=run)
+        def new_lo(step):
+            lo[step] = los.tile([P, 2 * HALF * PACK], BF16, name="lo", align_bytes=64)
 
-        def packed(tile, start, width, run):
-            return tile[:, start * PACK : (start + width) * PACK].rearrange("p (c i t) -> p c t i", t=PACK, i=run)
-
-        def routed(g):
-            return ROUTED.get(g, 0)
-
-        def halves_of(full):
-            halves = full[:].rearrange("p t w -> p (t w)").bitcast(BF16)
-            return halves.rearrange("p (t w e) -> p t w e", t=PACK, e=2)[:, :, :, 1]
-
-        def copies(g):
-            todo = []
-            hi[g] = his.tile([P, 2 * HALF * PACK], BF16, name="hi", align_bytes=64)
-            start = 0
-            for block in GROUPS[g]:
-                width = block[3]
-                full = full_hi if g == 0 else raw[block]
-                skip = routed(g) if start == 0 else 0
-                step = min(QUARTER, width - skip) if skip or g == 9 else width
-                for s in range(skip, width, step):
-                    todo.append((packed(hi[g], start + s, step, 4), runs(halves_of(full)[:, :, s : s + step], 4)))
-                start += width
-            return todo
-
-        def copy_upper_halves(g):
-            for dst, src in copies(g):
-                nc.scalar.copy(out=dst, in_=src)
-
-        negative, flipped, low_t, low_p = {}, {}, {}, {}
-
-        def negate_routed(g):
-            negative[g] = keep.tile([P, PACK, routed(g)], F32, name="negative_%d" % (g % 2))
-            nc.vector.tensor_scalar(
-                out=negative[g][:].bitcast(I32), in0=raw[GROUPS[g][0]][:, :, : routed(g)].bitcast(I32),
-                scalar1=MASK_F32, scalar2=SIGN, op0=ALU.bitwise_and, op1=ALU.bitwise_xor,
-            )
-
-        def route_there(g):
-            for s in range(0, routed(g), P):
-                flipped[g, s] = psum.tile([P, PACK * P], F32, name="bank_b%d" % (s // P))
-                for t in range(PACK):
-                    for source, first in ((raw[GROUPS[g][0]], True), (negative[g], False)):
-                        nc.tensor.matmul(
-                            flipped[g, s][:, t * P : (t + 1) * P], lhsT=source[:, t, s : s + P], rhs=eye_f32[:],
-                            start=first, stop=not first, is_transpose=True,
-                        )
-            nc.scalar.activation(packed(hi[g], 0, routed(g), 4), runs(halves_of(negative[g]), 4), ACT.Copy, scale=-1.0)
-
-        def route_back(g):
-            for s in range(0, routed(g), P):
-                low_t[g, s] = keep.tile([P, PACK * P], BF16, name="low_t_%d" % s)
-                nc.scalar.copy(out=low_t[g, s][:], in_=flipped[g, s][:])
-            for s in range(0, routed(g), P):
-                low_p[g, s] = psum.tile([P, PACK, P], BF16, name="bank_b%d" % ((s // P + max(2, routed(g) // P)) % 4))
-                for t in range(PACK):
-                    nc.tensor.transpose(low_p[g, s][:, t, :], low_t[g, s][:, t * P : (t + 1) * P], eye_bf16[:])
-
-        def route_end(g):
-            for s in range(0, routed(g), P):
-                nc.scalar.copy(
-                    out=lo[g][:, s * PACK : (s + P) * PACK].rearrange("p (c t) -> p c t", t=PACK),
-                    in_=low_p[g, s][:].rearrange("p t c -> p c t"),
-                )
+        first_hi = keep.tile([P, PACK, STEPS[0][0][3]], F32, name="first_hi")
 
         def mask_first():
             nc.vector.tensor_scalar(
-                out=full_hi[:].bitcast(I32), in0=raw[GROUPS[0][0]][:].bitcast(I32), scalar1=MASK_F32, scalar2=None, op0=ALU.bitwise_and
+                out=first_hi[:].bitcast(I32), in0=raw[STEPS[0][0]][:].bitcast(I32),
+                scalar1=MASK_F32, scalar2=None, op0=ALU.bitwise_and,
             )
 
-        def mask(g):
-            width = sum(block[3] for block in GROUPS[g])
-            bits = hi[g][:, routed(g) * PACK : width * PACK].bitcast(I32)
-            nc.vector.tensor_scalar(out=bits, in0=bits, scalar1=MASK_PAIR, scalar2=None, op0=ALU.bitwise_and)
+        def copy_next():
+            step = len(hi)
+            hi[step] = his.tile([P, 2 * HALF * PACK], BF16, name="hi", align_bytes=64)
+            start = 0
+            for i, block in enumerate(STEPS[step]):
+                skip = DETOUR if takes_detour(step) and i == 0 else 0
+                source = upper_halves(first_hi if step == 0 else raw[block])[:, :, skip:]
+                nc.scalar.copy(
+                    out=packed_by_runs(hi[step], start + skip, block[3] - skip, COPY_RUN), in_=by_runs(source, COPY_RUN)
+                )
+                start += block[3]
 
-        def subtract(g, i, parts):
-            if i == 0:
-                lo[g] = los.tile([P, 2 * HALF * PACK], BF16, name="lo", align_bytes=64)
-            block = GROUPS[g][i]
-            begin = sum(other[3] for other in GROUPS[g][:i])
-            skip = routed(g) if i == 0 else 0
-            step = (block[3] - skip) // parts
-            for s in range(skip, block[3], step):
-                minus = runs(full_hi[:], 2) if g == 0 else packed(hi[g], begin + s, step, 2)
+        def mask(step):
+            skip = DETOUR if takes_detour(step) else 0
+            pairs = hi[step][:, skip * PACK : columns(STEPS[step]) * PACK].bitcast(I32)
+            nc.vector.tensor_scalar(out=pairs, in0=pairs, scalar1=MASK_BF16_PAIR, scalar2=None, op0=ALU.bitwise_and)
+
+        def subtract(step, i, parts=1):
+            block = STEPS[step][i]
+            start = columns(STEPS[step][:i])
+            skip = DETOUR if takes_detour(step) and i == 0 else 0
+            width = (block[3] - skip) // parts
+            for s in range(skip, block[3], width):
+                high = by_runs(first_hi[:], SUBTRACT_RUN) if step == 0 else packed_by_runs(hi[step], start + s, width, SUBTRACT_RUN)
                 nc.vector.tensor_tensor(
-                    out=packed(lo[g], begin + s, step, 2), in0=runs(raw[block][:, :, s : s + step], 2), in1=minus, op=ALU.subtract
+                    out=packed_by_runs(lo[step], start + s, width, SUBTRACT_RUN),
+                    in0=by_runs(raw[block][:, :, s : s + width], SUBTRACT_RUN), in1=high, op=ALU.subtract,
+                )
+
+        negative, sums, back = {}, {}, {}
+
+        def negate(step):
+            negative[step] = keep.tile([P, PACK, DETOUR], F32, name="negative_%d" % (step % 2))
+            nc.vector.tensor_scalar(
+                out=negative[step][:].bitcast(I32), in0=raw[STEPS[step][0]][:, :, :DETOUR].bitcast(I32),
+                scalar1=MASK_F32, scalar2=SIGN_F32, op0=ALU.bitwise_and, op1=ALU.bitwise_xor,
+            )
+
+        def detour_start(step):
+            for i, s in enumerate(range(0, DETOUR, P)):
+                sums[step, i] = psum.tile([P, PACK * P], F32, name="bank_b%d" % i)
+                for t in range(PACK):
+                    for source, first in ((raw[STEPS[step][0]], True), (negative[step], False)):
+                        nc.tensor.matmul(
+                            sums[step, i][:, t * P : (t + 1) * P], lhsT=source[:, t, s : s + P], rhs=eye_f32[:],
+                            start=first, stop=not first, is_transpose=True,
+                        )
+            nc.scalar.activation(
+                packed_by_runs(hi[step], 0, DETOUR, COPY_RUN), by_runs(upper_halves(negative[step]), COPY_RUN), ACT.Copy, scale=-1.0
+            )
+
+        def detour_back(step):
+            tiles = range(DETOUR // P)
+            turned = {}
+            for i in tiles:
+                turned[i] = keep.tile([P, PACK * P], BF16, name="turned_%d" % i)
+                nc.scalar.copy(out=turned[i][:], in_=sums[step, i][:])
+            for i in tiles:
+                back[step, i] = psum.tile([P, PACK, P], BF16, name="bank_b%d" % (len(tiles) + i))
+                for t in range(PACK):
+                    nc.tensor.transpose(back[step, i][:, t, :], turned[i][:, t * P : (t + 1) * P], eye_bf16[:])
+
+        def detour_end(step):
+            for i, s in enumerate(range(0, DETOUR, P)):
+                nc.scalar.copy(
+                    out=lo[step][:, s * PACK : (s + P) * PACK].rearrange("p (c t) -> p c t", t=PACK),
+                    in_=back[step, i][:].rearrange("p t c -> p c t"),
                 )
 
         def quantize(tile, part, blocks, start, parts=1):
-            side, col = home(blocks[0])
+            side, first = home(blocks[0])
             c = blocks[0][1]
-            width = sum(block[3] for block in blocks)
-            step = width // parts
-            for s in range(0, width, step):
-                dst = slice(col + s, col + s + step)
+            width = columns(blocks) // parts
+            for s in range(0, columns(blocks), width):
+                cols = slice(first + s, first + s + width)
                 nc.vector.quantize_mx(
-                    out=codes[side, part, c][:, dst].bitcast(FP8X4),
-                    scales=scales[side, part, c][:, dst],
-                    in_=tile[:, (start + s) * PACK : (start + s + step) * PACK],
+                    out=codes[side, part, c][:, cols].bitcast(FP8X4),
+                    scales=scales[side, part, c][:, cols],
+                    in_=tile[:, (start + s) * PACK : (start + s + width) * PACK],
                 )
 
         banks = {}
 
-        def open_banks(c0, width, tag):
+        def open_banks(first, width, tag):
             for m in range(M_TILES):
-                banks[c0, m] = psum.tile([P, width], F32, name="bank_%s%d" % (tag, m))
+                banks[first, m] = psum.tile([P, width], F32, name="bank_%s%d" % (tag, m))
 
-        def multiply(block, pairs):
-            src, c, c0, width = block
-            if c0 < HALF:
-                starts, n = [0] if c0 + width == HALF else [], HALF
+        def multiply(block, products):
+            c, first, width = block[1:]
+            if first < HALF:
+                starts, n = [0] if first + width == HALF else [], HALF
             else:
-                starts, n = range(c0, c0 + width, QUARTER), QUARTER
+                starts, n = range(first, first + width, QUARTER), QUARTER
             for n0 in starts:
                 side, col = home(("x", c, n0, n))
                 for m in range(M_TILES):
-                    w_cols = slice(m * P, (m + 1) * P)
-                    x_cols = slice(col, col + n)
-                    for w_part, x_part in pairs:
+                    for w_part, x_part in products:
                         nc.tensor.matmul_mx(
                             out=banks[n0, m][:],
-                            lhsT=codes["left", w_part, c][:, w_cols].bitcast(FP8X4),
-                            lhsT_scale=scales["left", w_part, c][:, w_cols],
-                            rhs=codes[side, x_part, c][:, x_cols].bitcast(FP8X4),
-                            rhs_scale=scales[side, x_part, c][:, x_cols],
+                            lhsT=codes["left", w_part, c][:, m * P : (m + 1) * P].bitcast(FP8X4),
+                            lhsT_scale=scales["left", w_part, c][:, m * P : (m + 1) * P],
+                            rhs=codes[side, x_part, c][:, col : col + n].bitcast(FP8X4),
+                            rhs_scale=scales[side, x_part, c][:, col : col + n],
                             start=(c == 0 and (w_part, x_part) == ("hi", "hi")),
                             stop=(c == PASSES - 1 and (w_part, x_part) == ("hi", "lo")),
                         )
 
-        def drain(c0, width, vector_tiles):
+        def store(first, width, vector_tiles):
             for m in range(M_TILES):
-                res = keep.tile([P, width], F32, name="res_%d_%d" % (c0, m))
+                result = keep.tile([P, width], F32, name="result_%d_%d" % (first, m))
                 if m in vector_tiles:
-                    nc.vector.tensor_scalar(out=res[:], in0=banks[c0, m][:], scalar1=bias[:, m : m + 1], scalar2=None, op0=ALU.add)
+                    nc.vector.tensor_scalar(
+                        out=result[:], in0=banks[first, m][:], scalar1=bias[:, m : m + 1], scalar2=None, op0=ALU.add
+                    )
                 else:
-                    nc.scalar.activation(res[:], banks[c0, m][:], ACT.Identity, bias=bias[:, m : m + 1])
-                nc.sync.dma_start(out=out[m * P : (m + 1) * P, c0 : c0 + width], in_=res[:])
+                    nc.scalar.activation(result[:], banks[first, m][:], ACT.Identity, bias=bias[:, m : m + 1])
+                nc.sync.dma_start(out=out[m * P : (m + 1) * P, first : first + width], in_=result[:])
 
-        def finish_low(g, parts=1):
-            block = GROUPS[g][-1]
-            quantize(lo[g], "lo", [block], sum(other[3] for other in GROUPS[g][:-1]), parts)
-            if block[0] == "x":
+        def finish(step, parts=1):
+            block = STEPS[step][-1]
+            quantize(lo[step], "lo", [block], columns(STEPS[step][:-1]), parts)
+            operand, c, first = block[:3]
+            if operand == "x":
                 multiply(block, [("hi", "lo")])
-                if block[1] == PASSES - 1:
-                    if block[2] == 0:
-                        drain(0, HALF, ())
+                if c == PASSES - 1:
+                    if first == 0:
+                        store(0, HALF, ())
                         open_banks(HALF + QUARTER, QUARTER, "a")
                         open_banks(HALF, QUARTER, "b")
-                    elif block[2] == HALF:
-                        drain(HALF, QUARTER, ())
+                    elif first == HALF:
+                        store(HALF, QUARTER, ())
                     else:
-                        drain(HALF + QUARTER, QUARTER, (1, 3))
+                        store(HALF + QUARTER, QUARTER, (1, 3))
 
         open_banks(0, HALF, "a")
-        last = len(GROUPS) - 1
         mask_first()
-        copy_upper_halves(0)
-        copy_upper_halves(1)
-        copy_upper_halves(2)
-        subtract(0, 0, 1)
-        quantize(hi[0], "hi", GROUPS[0], 0)
-        for g in range(1, last + 1):
-            pair = len(GROUPS[g]) == 2
-            block = GROUPS[g][-1]
-            ahead = []
-            if routed(g):
-                if g not in negative:
-                    negate_routed(g)
-                    route_there(g)
-                ahead = copies(max(hi) + 1) if max(hi) < g + 2 else []
-            elif g + 2 <= last and g != 9 and g + 2 not in hi and not (routed(g + 1) and g + 2 > 6):
-                if not (g == 5 and routed(7) and False):
-                    copy_upper_halves(g + 2)
-            elif g == 9:
-                copy_upper_halves(10)
-            mask(g)
-            finish_low(g - 1)
-            if g == 9:
-                copy_upper_halves(11)
-            if routed(g):
-                route_back(g)
-                for dst, src in ahead[: AHEAD[g]]:
-                    nc.scalar.copy(out=dst, in_=src)
-                subtract(g, 0, 1)
-                route_end(g)
-                for dst, src in ahead[AHEAD[g] :]:
-                    nc.scalar.copy(out=dst, in_=src)
-            if g < last and routed(g + 1):
-                negate_routed(g + 1)
-                route_there(g + 1)
-            quantize(hi[g], "hi", GROUPS[g], 0)
-            if block[0] == "x":
-                multiply(block, [("hi", "hi")] if pair else [("hi", "hi"), ("lo", "hi")])
-            if pair:
-                if not routed(g):
-                    subtract(g, 0, 1)
-                subtract(g, 1, 1)
-                quantize(lo[g], "lo", GROUPS[g][:1], 0)
-                multiply(block, [("lo", "hi")])
-            elif not routed(g):
-                subtract(g, 0, 2 if g == last else 1)
-        finish_low(last, 2)
+        copy_next()
+        copy_next()
+        copy_next()
+        new_lo(0)
+        subtract(0, 0)
+        quantize(hi[0], "hi", STEPS[0], 0)
+        for step in range(1, LAST + 1):
+            blocks = STEPS[step]
+            wanted = 0 if takes_detour(step) or takes_detour(step + 1) else min(step + 3, LAST + 1)
+            if len(hi) < wanted:
+                copy_next()
+            mask(step)
+            finish(step - 1)
+            if len(hi) < wanted:
+                copy_next()
+
+            new_lo(step)
+            if takes_detour(step):
+                detour_back(step)
+                copy_next()
+                subtract(step, 0)
+                detour_end(step)
+            if takes_detour(step + 1):
+                negate(step + 1)
+                detour_start(step + 1)
+
+            quantize(hi[step], "hi", blocks, 0)
+            x_block = blocks[-1]
+            if takes_detour(step):
+                multiply(x_block, [("hi", "hi")])
+                subtract(step, 1)
+                quantize(lo[step], "lo", blocks[:1], 0)
+                multiply(x_block, [("lo", "hi")])
+            else:
+                if x_block[0] == "x":
+                    multiply(x_block, [("hi", "hi"), ("lo", "hi")])
+                subtract(step, 0, 2 if step == LAST else 1)
+        finish(LAST, 2)

from contextlib import ExitStack

import concourse.mybir as mybir
from concourse.masks import make_identity

K, M, T = 2048, 512, 1024
FLOPS = 3 * 2 * K * M * T

F32 = mybir.dt.float32
BF16 = mybir.dt.bfloat16
I32 = mybir.dt.int32
U32 = mybir.dt.uint32
U8 = mybir.dt.uint8
FP8X4 = mybir.dt.float8_e4m3fn_x4
ALU = mybir.AluOpType
ACT = mybir.ActivationFunctionType

P = 128
PACK = 4
K_PASS = P * PACK
PASSES = K // K_PASS
M_TILES = M // P
HALF = T // 2
QUARTER = T // 4

MASK_F32 = 0xFFF00000 - 2**32
MASK_BF16_PAIR = 0xFFF0FFF0 - 2**32
SIGN_F32 = -(2**31)

STEPS = (
    (("w", 0, 0, 128),),
    (("w", 0, 128, 128),),
    (("w", 0, 256, 256),),
    (("x", 0, 0, 256),),
    (("x", 0, 256, 256),),
    (("w", 1, 0, 512),),
    (("x", 1, 0, 512),),
    (("w", 2, 0, 512), ("x", 2, 0, 512)),
    (("w", 3, 0, 512), ("x", 3, 0, 512)),
    (("x", 0, 512, 512),),
    (("x", 1, 512, 512),),
    (("x", 2, 512, 512),),
    (("x", 3, 512, 256),),
    (("x", 3, 768, 256),),
)
LAST = len(STEPS) - 1
DETOUR = 256
BIAS_AHEAD_OF = ("x", 2, 512, 512)
COPY_RUN = 4
SUBTRACT_RUN = 2


def takes_detour(step):
    return step <= LAST and len(STEPS[step]) == 2


def columns(blocks):
    return sum(block[3] for block in blocks)


def home(block):
    operand, first = block[0], block[2]
    if operand == "w":
        return "left", first
    return ("left", M + first) if first < HALF else ("right", first - HALF)


def by_runs(rows, run):
    return rows.rearrange("p t (c i) -> p c t i", i=run)


def packed_by_runs(tile, start, width, run):
    return tile[:, start * PACK : (start + width) * PACK].rearrange("p (c i t) -> p c t i", t=PACK, i=run)


def upper_halves(full):
    halves = full[:].rearrange("p t w -> p (t w)").bitcast(BF16)
    return halves.rearrange("p (t w e) -> p t w e", t=PACK, e=2)[:, :, :, 1]


def tile_mix_split3_fm_bias_kernel(tc, w, x, b, out):
    nc = tc.nc
    with ExitStack() as ctx:
        ctx.enter_context(tc.manual_schedule())
        keep = ctx.enter_context(tc.tile_pool(name="keep", bufs=1))
        his = ctx.enter_context(tc.tile_pool(name="his", bufs=3))
        los = ctx.enter_context(tc.tile_pool(name="los", bufs=2))
        psum = ctx.enter_context(tc.psum_pool(name="psum", bufs=1))

        table_in = keep.tile([P, 8], F32, name="table_in")
        table_out = keep.tile([P, 8], F32, name="table_out")
        nc.vector.memset(table_in[:], 0.0)
        nc.scalar.activation(table_out[:], table_in[:], ACT.Identity)

        eye_f32 = keep.tile([P, P], F32, name="eye_f32")
        eye_bf16 = keep.tile([P, P], BF16, name="eye_bf16")
        make_identity(nc, eye_f32[:])
        make_identity(nc, eye_bf16[:])

        bias = keep.tile([P, M_TILES], F32, name="bias")
        raw = {}
        for block in [block for blocks in STEPS for block in blocks]:
            operand, c, first, width = block
            if block == BIAS_AHEAD_OF:
                with nc.allow_non_contiguous_dma(reason="one bias value to a partition"):
                    nc.sync.dma_start(out=bias[:], in_=b.rearrange("(m p) -> p m", p=P))
            raw[block] = keep.tile([P, PACK, width], F32, name="raw_%s_%d_%d" % (operand, c, first))
            rows = (w if operand == "w" else x)[c * K_PASS : (c + 1) * K_PASS, first : first + width]
            nc.sync.dma_start(out=raw[block][:], in_=rows.rearrange("(p j) w -> p j w", j=PACK))

        codes, scales = {}, {}
        for c in range(PASSES):
            for side, width in (("left", M + HALF), ("right", HALF)):
                for part in ("hi", "lo"):
                    tag = "%s_%s_%d" % (side, part, c)
                    codes[side, part, c] = keep.tile([P, width], U32, name="codes_" + tag, align_bytes=64)
                    scales[side, part, c] = keep.tile([P, width], U8, name="scales_" + tag, align_bytes=64)

        hi, lo = {}, {}

        def new_lo(step):
            lo[step] = los.tile([P, 2 * HALF * PACK], BF16, name="lo", align_bytes=64)

        first_hi = keep.tile([P, PACK, STEPS[0][0][3]], F32, name="first_hi")

        def mask_first():
            nc.vector.tensor_scalar(
                out=first_hi[:].bitcast(I32), in0=raw[STEPS[0][0]][:].bitcast(I32),
                scalar1=MASK_F32, scalar2=None, op0=ALU.bitwise_and,
            )

        def copy_next():
            step = len(hi)
            hi[step] = his.tile([P, 2 * HALF * PACK], BF16, name="hi", align_bytes=64)
            start = 0
            for i, block in enumerate(STEPS[step]):
                skip = DETOUR if takes_detour(step) and i == 0 else 0
                source = upper_halves(first_hi if step == 0 else raw[block])[:, :, skip:]
                nc.scalar.copy(
                    out=packed_by_runs(hi[step], start + skip, block[3] - skip, COPY_RUN), in_=by_runs(source, COPY_RUN)
                )
                start += block[3]

        def mask(step):
            skip = DETOUR if takes_detour(step) else 0
            pairs = hi[step][:, skip * PACK : columns(STEPS[step]) * PACK].bitcast(I32)
            nc.vector.tensor_scalar(out=pairs, in0=pairs, scalar1=MASK_BF16_PAIR, scalar2=None, op0=ALU.bitwise_and)

        def subtract(step, i, parts=1):
            block = STEPS[step][i]
            start = columns(STEPS[step][:i])
            skip = DETOUR if takes_detour(step) and i == 0 else 0
            width = (block[3] - skip) // parts
            for s in range(skip, block[3], width):
                high = by_runs(first_hi[:], SUBTRACT_RUN) if step == 0 else packed_by_runs(hi[step], start + s, width, SUBTRACT_RUN)
                nc.vector.tensor_tensor(
                    out=packed_by_runs(lo[step], start + s, width, SUBTRACT_RUN),
                    in0=by_runs(raw[block][:, :, s : s + width], SUBTRACT_RUN), in1=high, op=ALU.subtract,
                )

        negative, sums, back = {}, {}, {}

        def negate(step):
            negative[step] = keep.tile([P, PACK, DETOUR], F32, name="negative_%d" % (step % 2))
            nc.vector.tensor_scalar(
                out=negative[step][:].bitcast(I32), in0=raw[STEPS[step][0]][:, :, :DETOUR].bitcast(I32),
                scalar1=MASK_F32, scalar2=SIGN_F32, op0=ALU.bitwise_and, op1=ALU.bitwise_xor,
            )

        def detour_start(step):
            for i, s in enumerate(range(0, DETOUR, P)):
                sums[step, i] = psum.tile([P, PACK * P], F32, name="bank_b%d" % i)
                for t in range(PACK):
                    for source, first in ((raw[STEPS[step][0]], True), (negative[step], False)):
                        nc.tensor.matmul(
                            sums[step, i][:, t * P : (t + 1) * P], lhsT=source[:, t, s : s + P], rhs=eye_f32[:],
                            start=first, stop=not first, is_transpose=True,
                        )
            nc.scalar.activation(
                packed_by_runs(hi[step], 0, DETOUR, COPY_RUN), by_runs(upper_halves(negative[step]), COPY_RUN), ACT.Copy, scale=-1.0
            )

        def detour_back(step):
            tiles = range(DETOUR // P)
            turned = {}
            for i in tiles:
                turned[i] = keep.tile([P, PACK * P], BF16, name="turned_%d" % i)
                nc.scalar.copy(out=turned[i][:], in_=sums[step, i][:])
            for i in tiles:
                back[step, i] = psum.tile([P, PACK, P], BF16, name="bank_b%d" % (len(tiles) + i))
                for t in range(PACK):
                    nc.tensor.transpose(back[step, i][:, t, :], turned[i][:, t * P : (t + 1) * P], eye_bf16[:])

        def detour_end(step):
            for i, s in enumerate(range(0, DETOUR, P)):
                nc.scalar.copy(
                    out=lo[step][:, s * PACK : (s + P) * PACK].rearrange("p (c t) -> p c t", t=PACK),
                    in_=back[step, i][:].rearrange("p t c -> p c t"),
                )

        def quantize(tile, part, blocks, start, parts=1):
            side, first = home(blocks[0])
            c = blocks[0][1]
            width = columns(blocks) // parts
            for s in range(0, columns(blocks), width):
                cols = slice(first + s, first + s + width)
                nc.vector.quantize_mx(
                    out=codes[side, part, c][:, cols].bitcast(FP8X4),
                    scales=scales[side, part, c][:, cols],
                    in_=tile[:, (start + s) * PACK : (start + s + width) * PACK],
                )

        banks = {}

        def open_banks(first, width, tag):
            for m in range(M_TILES):
                banks[first, m] = psum.tile([P, width], F32, name="bank_%s%d" % (tag, m))

        def multiply(block, products):
            c, first, width = block[1:]
            if first < HALF:
                starts, n = [0] if first + width == HALF else [], HALF
            else:
                starts, n = range(first, first + width, QUARTER), QUARTER
            for n0 in starts:
                side, col = home(("x", c, n0, n))
                for m in range(M_TILES):
                    for w_part, x_part in products:
                        nc.tensor.matmul_mx(
                            out=banks[n0, m][:],
                            lhsT=codes["left", w_part, c][:, m * P : (m + 1) * P].bitcast(FP8X4),
                            lhsT_scale=scales["left", w_part, c][:, m * P : (m + 1) * P],
                            rhs=codes[side, x_part, c][:, col : col + n].bitcast(FP8X4),
                            rhs_scale=scales[side, x_part, c][:, col : col + n],
                            start=(c == 0 and (w_part, x_part) == ("hi", "hi")),
                            stop=(c == PASSES - 1 and (w_part, x_part) == ("hi", "lo")),
                        )

        def store(first, width, vector_tiles):
            for m in range(M_TILES):
                result = keep.tile([P, width], F32, name="result_%d_%d" % (first, m))
                if m in vector_tiles:
                    nc.vector.tensor_scalar(
                        out=result[:], in0=banks[first, m][:], scalar1=bias[:, m : m + 1], scalar2=None, op0=ALU.add
                    )
                else:
                    nc.scalar.activation(result[:], banks[first, m][:], ACT.Identity, bias=bias[:, m : m + 1])
                nc.sync.dma_start(out=out[m * P : (m + 1) * P, first : first + width], in_=result[:])

        def finish(step, parts=1):
            block = STEPS[step][-1]
            quantize(lo[step], "lo", [block], columns(STEPS[step][:-1]), parts)
            operand, c, first = block[:3]
            if operand == "x":
                multiply(block, [("hi", "lo")])
                if c == PASSES - 1:
                    if first == 0:
                        store(0, HALF, ())
                        open_banks(HALF + QUARTER, QUARTER, "a")
                        open_banks(HALF, QUARTER, "b")
                    elif first == HALF:
                        store(HALF, QUARTER, ())
                    else:
                        store(HALF + QUARTER, QUARTER, (1, 3))

        open_banks(0, HALF, "a")
        mask_first()
        copy_next()
        copy_next()
        copy_next()
        new_lo(0)
        subtract(0, 0)
        quantize(hi[0], "hi", STEPS[0], 0)
        for step in range(1, LAST + 1):
            blocks = STEPS[step]
            wanted = 0 if takes_detour(step) or takes_detour(step + 1) else min(step + 3, LAST + 1)
            if len(hi) < wanted:
                copy_next()
            mask(step)
            finish(step - 1)
            if len(hi) < wanted:
                copy_next()

            new_lo(step)
            if takes_detour(step):
                detour_back(step)
                copy_next()
                subtract(step, 0)
                detour_end(step)
            if takes_detour(step + 1):
                negate(step + 1)
                detour_start(step + 1)

            quantize(hi[step], "hi", blocks, 0)
            x_block = blocks[-1]
            if takes_detour(step):
                multiply(x_block, [("hi", "hi")])
                subtract(step, 1)
                quantize(lo[step], "lo", blocks[:1], 0)
                multiply(x_block, [("lo", "hi")])
            else:
                if x_block[0] == "x":
                    multiply(x_block, [("hi", "hi"), ("lo", "hi")])
                subtract(step, 0, 2 if step == LAST else 1)
        finish(LAST, 2)
